import numpy as np
import ml_dtypes

BF16 = ml_dtypes.bfloat16


def bf(x):
    return np.asarray(x, np.float32).astype(BF16)


def f32(x):
    return np.asarray(x, np.float32)


def f64(x):
    return np.asarray(x).astype(np.float64)


def striped(idx):
    return np.concatenate([l.reshape(-1, 16).T for l in idx])


def rows(idx, k):
    return np.tile(np.repeat(idx, 16, axis=0), (k // (16 * 8), 1))


def look(tab, idx):
    return np.take_along_axis(f64(tab), rows(idx, len(tab)), axis=1)


K, S, D, V, N = 128, 2048, 2, 1024, 2048


def setup_inputs():
    return {"tab": f32(np.random.standard_normal((K, S))), "x0": f32(1.0 * np.random.standard_normal((K, V))), "offs": striped(np.stack([np.random.permutation(S)[:N] for _ in range(8)]))}


def reference(tab, x0, offs):
    idx = np.stack([g.T.reshape(-1) for g in np.split(offs, 8)])
    a = (f64(x0) + sum(look(tab, idx[:, d * V:(d + 1) * V]) for d in range(D))) / (D + 1)
    x = ((f64(x0) - a) ** 2 + sum((look(tab, idx[:, d * V:(d + 1) * V]) - a) ** 2 for d in range(D))) / (D + 1)
    return x

import math

import concourse.mybir as mybir

F32 = mybir.dt.float32
U16 = mybir.dt.uint16
ADD = mybir.AluOpType.add
SUBTRACT = mybir.AluOpType.subtract
COPY = mybir.ActivationFunctionType.Copy
SQUARE = mybir.ActivationFunctionType.Square

PIECE = 512
LANES = 16


def tile_lookup_vari_out_kernel(tc, tab, x0, offs, out):
    nc = tc.nc
    rows, nodes = x0.shape
    neighbours = offs.shape[1] * LANES // nodes
    members = neighbours + 1
    pieces = nodes // PIECE

    with tc.tile_pool(name="held", bufs=1) as held:

        def piece_tile(name):
            return held.tile([rows, PIECE], F32, name=name)

        def columns(p):
            return slice(p * PIECE, (p + 1) * PIECE)

        offsets = held.tile(list(offs.shape), U16, name="offsets")
        table = held.tile(list(tab.shape), F32, name="table")
        own = [piece_tile(f"own{p}") for p in range(pieces)]
        nc.sync.dma_start(offsets[:], offs)
        nc.scalar.dma_start(own[0][:], x0[:, columns(0)])
        nc.sync.dma_start(table[:], tab)
        for p in range(1, pieces):
            nc.sync.dma_start(own[p][:], x0[:, columns(p)])

        def neighbour(d, p):
            first = (d * nodes + p * PIECE) // LANES
            return table[:].indirect(offsets[:, first : first + PIECE // LANES])

        means = []
        for p in range(pieces):
            total = own[p]
            for d in range(neighbours):
                grown = piece_tile(f"total{p}_{d}")
                nc.vector.tensor_tensor(grown[:], neighbour(d, p), total[:], ADD)
                total = grown
            mean = piece_tile(f"mean{p}")
            nc.scalar.activation(mean[:], total[:], COPY, scale=1.0 / members)
            means.append(mean)

        for p in range(pieces):
            squares = []
            for m in range(members):
                value = own[p][:] if m == 0 else neighbour(m - 1, p)
                diff = piece_tile(f"diff{p}_{m}")
                nc.vector.tensor_tensor(diff[:], value, means[p][:], SUBTRACT)
                square = piece_tile(f"square{p}_{m}")
                nc.scalar.activation(square[:], diff[:], SQUARE, scale=1.0 / math.sqrt(members))
                squares.append(square)
            variance = squares[0]
            for m in range(1, members):
                grown = piece_tile(f"variance{p}_{m}")
                nc.vector.tensor_tensor(grown[:], variance[:], squares[m][:], ADD)
                variance = grown
            nc.sync.dma_start(out[:, columns(p)], variance[:])
